import numpy as np
import ml_dtypes


def mxq(x, axis, fmt="e4m3"):
    dtype, down = {"e4m3": (ml_dtypes.float8_e4m3fn, 7), "e5m2": (ml_dtypes.float8_e5m2, 14)}[fmt]
    v = np.moveaxis(np.asarray(x, np.float32).astype(ml_dtypes.bfloat16).astype(np.float64), axis, -1)
    blocks = v.reshape(v.shape[:-1] + (-1, 32))
    amax = np.abs(blocks).max(-1, keepdims=True)
    byte = np.maximum(np.where(amax > 0, np.frexp(amax)[1] - 1 + 127, 0) - down, 1)
    scale = np.exp2(byte - 127.0)
    codes = (blocks / scale).astype(np.float32).astype(dtype).astype(np.float64)
    return np.moveaxis((codes * scale).reshape(v.shape), -1, axis)


WIDE = False


def mx_kscale(k):
    if not WIDE:
        return np.ones(k)
    levels = np.array([10, -10, 5, -5, 0])
    if k % 512:
        return np.exp2(np.random.permutation(np.resize(levels, k // 32))).repeat(32)
    a = np.empty((k // 512, 16))
    for p in range(k // 512):
        a[p, :8] = np.random.permutation(np.resize(levels, 8))
        for g in range(8):
            far = levels[np.abs(levels - a[p, g]) >= 10]
            a[p, g + 8] = far[np.random.randint(len(far))]
    return np.exp2(a.ravel()).repeat(32)


def f64(x):
    return np.asarray(x).astype(np.float64)


def striped8(idx):
    return np.asarray(idx).reshape(8, -1, 16).transpose(0, 2, 1).reshape(128, -1).astype(np.uint16)


def unstriped8(offs):
    return offs.reshape(8, 16, -1).transpose(0, 2, 1).reshape(8, -1).astype(np.int64)


def pick8(x, idx, run):
    r = np.arange(len(x))
    return x[r[:, None], idx[r % (8 * run) // run]]


E2M1 = np.array([0.0, 0.5, 1.0, 1.5, 2.0, 3.0, 4.0, 6.0, -0.0, -0.5, -1.0, -1.5, -2.0, -3.0, -4.0, -6.0])


def pack_weight(w, fmt):
    k, n = w.shape
    w = f64(np.asarray(w, np.float32).astype(ml_dtypes.bfloat16)).reshape(k // 32, 32, n)
    amax = np.abs(w).max(1)
    if fmt == "e4m3":
        byte = np.frexp(amax)[1] - 1 + 127 - 7
    else:
        mant, ex = np.frexp(amax / 6.0)
        byte = np.where(mant > 0.5, ex, ex - 1) + 127
    byte = np.clip(np.where(amax > 0, byte, 1), 1, 254)
    scaled = (w * np.exp2(127.0 - byte)[:, None, :]).reshape(k, n).astype(np.float32)
    by_word = np.ascontiguousarray(scaled.reshape(k // 512, 128, 4, n).transpose(0, 1, 3, 2))
    if fmt == "e4m3":
        words = by_word.astype(ml_dtypes.float8_e4m3fn).view(np.uint8)
    else:
        c = by_word.astype(ml_dtypes.float4_e2m1fn).view(np.uint8) & 0xF
        words = (c[..., 0::2] | (c[..., 1::2] << 4)).reshape(k // 512, 128, 2 * n)
    return np.ascontiguousarray(words), np.ascontiguousarray(byte.astype(np.uint8).reshape(k // 512, 16, n))


def unpack_weight(words, scales, fmt):
    g, _, n = scales.shape
    words = np.ascontiguousarray(words).reshape(g, 128, n, -1)
    if fmt == "e4m3":
        vals = words.view(ml_dtypes.float8_e4m3fn).astype(np.float64)
    else:
        nib = np.empty((g, 128, n, 4), np.uint8)
        nib[..., 0::2] = words & 0xF
        nib[..., 1::2] = words >> 4
        vals = E2M1[nib]
    vals = vals * np.repeat(np.exp2(scales.astype(np.float64) - 127.0), 8, axis=1)[..., None]
    return vals.transpose(0, 1, 3, 2).reshape(g * 512, n)


D, V, Q, I, G = 512, 2048, 128, 512, 64


def setup_inputs():
    n = np.random.standard_normal
    idx = np.stack([np.random.permutation(V)[:I] for _ in range(8)])
    fd = mx_kscale(D)
    vocp = pack_weight(n((D, V)) / fd[:, None], "e4m3")
    return {
        "hid": (n((D, Q)) * 1.0 / np.sqrt(D) * fd[:, None]).astype(np.float32),
        "voc_words": vocp[0],
        "voc_scales": vocp[1],
        "target": (np.random.uniform(0.0, 0.1, (Q, G))).astype(np.float32),
        "old": (0.5 * n((Q, V))).astype(np.float32),
        "offs": striped8(idx),
    }


def reference(hid, voc_words, voc_scales, target, old, offs):
    idx = unstriped8(offs)
    vocu = unpack_weight(voc_words, voc_scales, "e4m3")
    hidq = mxq(f64(hid), 0, "e4m3")
    a = hidq.T @ vocu
    m1 = np.max(a, axis=1, keepdims=True)
    p = np.exp(a - m1)
    z = np.sum(p, axis=1, keepdims=True)
    px = np.exp(pick8(a, idx, 16) - m1)
    u1 = px.reshape(Q, G, I // G).sum(axis=2) / z
    du1 = f64(target) / u1
    e1 = du1 / z
    r1 = np.repeat(e1, I // G, axis=1)
    dz = np.sum(du1 * px.reshape(Q, G, I // G).sum(axis=2) / np.square(z) * (-1.0), axis=1, keepdims=True)
    e2 = r1 * px
    s2 = np.zeros((Q, V))
    s2[np.arange(Q)[:, None], idx[np.arange(Q) % 128 // 16]] = e2
    da = dz * p + s2
    y = da * 64.0 + f64(old)
    return y

@@ -1,0 +1,173 @@
+from contextlib import ExitStack
+
+import concourse.mybir as mybir
+from concourse.masks import make_identity
+
+F32 = mybir.dt.float32
+BF16 = mybir.dt.bfloat16
+I32 = mybir.dt.int32
+U32 = mybir.dt.uint32
+U16 = mybir.dt.uint16
+U8 = mybir.dt.uint8
+FP8X4 = mybir.dt.float8_e4m3fn_x4
+ALU = mybir.AluOpType
+ACT = mybir.ActivationFunctionType
+AX = mybir.AxisListType
+
+P = 128
+D, V, Q, I, G = 512, 2048, 128, 512, 64
+PACK = 4
+GROUP = I // G
+N = 512
+CH = V // N
+OUT_SCALE = 64.0
+FLOPS = 2 * D * Q * V
+WORD_LOADS = [(0, 512), (512, 1024), (1536, 512)]
+
+
+def tile_attend_bgroupshare_heads_kernel(tc, hid, voc_words, voc_scales, target, old, offs, out):
+    nc = tc.nc
+    with ExitStack() as ctx:
+        sb = ctx.enter_context(tc.tile_pool(name="sb", bufs=1))
+        ps = ctx.enter_context(tc.psum_pool(name="ps", bufs=1))
+
+        hid_raw = sb.tile([P, PACK, Q], F32, name="hid_raw")
+        nc.sync.dma_start(hid_raw[:], hid.rearrange("(p j) q -> p j q", j=PACK))
+
+        planes = sb.tile([P, N], U8, name="planes", align_bytes=64)
+        for quad in range(4):
+            nc.sync.dma_start(
+                planes[32 * quad : 32 * quad + 16, :].bitcast(I32),
+                voc_scales[0][4 * quad : 4 * quad + 4, :].rearrange("r (c n) -> c r n", c=CH).bitcast(I32),
+            )
+
+        flat_words = voc_words[0].rearrange("p n t -> p (n t)")
+        word_of = {}
+        for first, width in WORD_LOADS:
+            wt = sb.tile([P, width], U32, name="words%d" % first, align_bytes=64)
+            nc.sync.dma_start(wt[:].bitcast(I32), flat_words[:, PACK * first : PACK * (first + width)].bitcast(I32))
+            for c0 in range(0, width, N):
+                word_of[(first + c0) // N] = wt[:, c0 : c0 + N]
+
+        offsets = sb.tile([P, I // 16], U16, name="offsets")
+        nc.sync.dma_start(offsets[:], offs)
+        tgt = sb.tile([P, G], F32, name="tgt")
+        nc.sync.dma_start(tgt[:], target)
+        olds = []
+        for h in range(2):
+            ot = sb.tile([P, V // 2], F32, name="old%d" % h)
+            nc.sync.dma_start(ot[:], old[:, h * (V // 2) : (h + 1) * (V // 2)])
+            olds.append(ot)
+
+        warm = sb.tile([P, 1], F32, name="warm")
+        nc.vector.memset(warm[:], 0.0)
+        warm_out = sb.tile([P, 1], F32, name="warm_out")
+        nc.scalar.activation(warm_out[:], warm[:], ACT.Exp)
+
+        ident = sb.tile([P, P], F32, name="ident")
+        make_identity(nc, ident[:])
+
+        s2 = sb.tile([P, V], F32, name="s2")
+        nc.vector.memset(s2[:], 0.0)
+        f = sb.tile([P, CH], F32, name="f")
+        nc.vector.memset(f[:, CH - 1 : CH], 1.0)
+
+        hid_bf = sb.tile([P, Q, PACK], BF16, name="hid_bf", align_bytes=64)
+        nc.vector.tensor_copy(hid_bf[:], hid_raw[:].rearrange("p j q -> p q j"))
+        hid_codes = sb.tile([P, Q], U32, name="hid_codes", align_bytes=64)
+        hid_scales = sb.tile([P, Q], U8, name="hid_scales", align_bytes=64)
+        nc.vector.quantize_mx(out=hid_codes[:].bitcast(FP8X4), scales=hid_scales[:], in_=hid_bf[:].rearrange("p q j -> p (q j)"))
+
+        tsum = sb.tile([P, 1], F32, name="tsum")
+        tneg = sb.tile([P, G], F32, name="tneg")
+        nc.scalar.activation(tneg[:], tgt[:], ACT.Copy, scale=-1.0, accum_out=tsum[:])
+
+        a = sb.tile([P, V], F32, name="a")
+        p = sb.tile([P, V], F32, name="p")
+        mx = sb.tile([P, CH], F32, name="mx")
+        zc = sb.tile([P, CH], F32, name="zc")
+        nm1 = sb.tile([P, 1], F32, name="nm1")
+        for c in range(CH):
+            cols = slice(c * N, (c + 1) * N)
+            bank = ps.tile([P, N], F32, name="bank%d" % c)
+            nc.tensor.matmul_mx(
+                out=bank[:],
+                lhsT=hid_codes[:].bitcast(FP8X4),
+                lhsT_scale=hid_scales[:],
+                rhs=word_of[c].bitcast(FP8X4),
+                rhs_scale=planes[4 * c : P, :],
+                start=True,
+                stop=True,
+            )
+            nc.vector.tensor_scalar(a[:, cols], bank[:], 1.0, None, ALU.mult, ALU.max, accum_out=mx[:, c : c + 1])
+            if c < CH - 1:
+                nm = sb.tile([P, 1], F32, name="nm%d" % c)
+                nc.gpsimd.tensor_scalar(nm[:], mx[:, c : c + 1], -1.0, 0.0, ALU.mult, ALU.add)
+            else:
+                nm = nm1
+                nc.vector.tensor_reduce(nm1[:], mx[:], AX.X, ALU.max, negate=True)
+                nc.scalar.activation(f[:, : CH - 1], mx[:, : CH - 1], ACT.Exp, bias=nm1[:])
+            nc.scalar.activation(p[:, cols], a[:, cols], ACT.Exp, bias=nm[:], accum_out=zc[:, c : c + 1])
+
+        ax = sb.tile([P, I], F32, name="ax")
+        nc.vector.tensor_copy(ax[:], a[:].indirect(offsets[:]))
+        H = I // 2
+        GH = G // 2
+        px = sb.tile([P, I], F32, name="px")
+        for h in range(2):
+            nc.scalar.activation(px[:, h * H : (h + 1) * H], ax[:, h * H : (h + 1) * H], ACT.Exp, bias=nm1[:])
+
+        zf = sb.tile([P, CH], F32, name="zf")
+        z = sb.tile([P, 1], F32, name="z")
+        nc.vector.scalar_tensor_tensor(zf[:], zc[:], 1.0 / OUT_SCALE, f[:], ALU.mult, ALU.mult, accum_out=z[:])
+        rz = sb.tile([P, 1], F32, name="rz")
+        nc.vector.reciprocal(rz[:], z[:])
+        cf = sb.tile([P, CH], F32, name="cf")
+        nc.vector.tensor_scalar(cf[:], f[:], rz[:], tsum[:], ALU.mult, ALU.mult)
+
+        gs = sb.tile([P, G], F32, name="gs")
+        rg = sb.tile([P, G], F32, name="rg")
+        r1 = sb.tile([P, I], F32, name="r1")
+        for h in range(2):
+            nc.vector.tensor_reduce(gs[:, h * GH : (h + 1) * GH], px[:, h * H : (h + 1) * H].rearrange("p (g j) -> p g j", j=GROUP), AX.X, ALU.add)
+        for h in range(2):
+            nc.vector.reciprocal(rg[:, h * GH : (h + 1) * GH], gs[:, h * GH : (h + 1) * GH])
+        for h in range(2):
+            nc.vector.scalar_tensor_tensor(
+                r1[:, h * H : (h + 1) * H].rearrange("p (g j) -> p g j", j=GROUP),
+                rg[:, h * GH : (h + 1) * GH].unsqueeze(2).to_broadcast([P, GH, GROUP]),
+                OUT_SCALE,
+                tgt[:, h * GH : (h + 1) * GH].unsqueeze(2).to_broadcast([P, GH, GROUP]),
+                ALU.mult,
+                ALU.mult,
+            )
+        nc.vector.tensor_tensor(s2[:].indirect(offsets[:]), px[:], r1[:], ALU.mult)
+
+        turned = []
+        for c in range(CH):
+            tb = ps.tile([P, N], F32, name="turned%d" % c)
+            for j in range(N // P):
+                o0 = (c % 2) * N + j * P
+                nc.tensor.matmul(tb[:, j * P : (j + 1) * P], olds[c // 2][:, o0 : o0 + P], ident[:], start=(j == 0), stop=False, is_transpose=True)
+            turned.append(tb)
+        for c in range(CH):
+            cols = slice(c * N, (c + 1) * N)
+            cp = sb.tile([P, N], F32, name="cp%d" % c)
+            nc.scalar.activation(cp[:], p[:, cols], ACT.Copy, scale=cf[:, c : c + 1])
+            for j in range(N // P):
+                nc.tensor.matmul(turned[c][:, j * P : (j + 1) * P], cp[:, j * P : (j + 1) * P], ident[:], start=False, stop=(j == N // P - 1), is_transpose=True)
+        backs = []
+        for c in range(CH):
+            wt = sb.tile([P, N], F32, name="wt%d" % c)
+            nc.scalar.copy(wt[:], turned[c][:])
+            back = ps.tile([P, N], F32, name="bank%d" % c)
+            for j in range(N // P):
+                nc.tensor.transpose(back[:, j * P : (j + 1) * P], wt[:, j * P : (j + 1) * P], ident[:])
+            backs.append(back)
+        first = 0
+        for k, width in enumerate([128, 384, 512, 512, 384, 128]):
+            cols = slice(first, first + width)
+            res = sb.tile([P, width], F32, name="res%d" % k)
+            nc.vector.tensor_tensor(res[:], backs[first // N][:, first % N : first % N + width], s2[:, cols], ALU.add)
+            (nc.sync if k % 2 == 0 else nc.scalar).dma_start(out[:, cols], res[:])
+            first = first + width

@@ -19,14 +19,19 @@ D, V, Q, I, G = 512, 2048, 128, 512, 64
 PACK = 4
 GROUP = I // G
 N = 512
-CH = V // N
+BANKS = V // N
 OUT_SCALE = 64.0
 FLOPS = 2 * D * Q * V
-WORD_LOADS = [(0, 512), (512, 1024), (1536, 512)]
+SCORE_CHUNKS = [(0, 512), (512, 512), (1024, 512), (1536, 512)]
+WORD_LOADS = [(0, 512), (512, 768), (1280, 768)]
+LIST_PIECES = [(0, 256), (256, 256)]
+DIRECT = 256
+STORE_WIDTHS = [256, 256, 512, 512, 512]
 
 
 def tile_attend_bgroupshare_heads_kernel(tc, hid, voc_words, voc_scales, target, old, offs, out):
     nc = tc.nc
+    CH = len(SCORE_CHUNKS)
     with ExitStack() as ctx:
         sb = ctx.enter_context(tc.tile_pool(name="sb", bufs=1))
         ps = ctx.enter_context(tc.psum_pool(name="ps", bufs=1))
@@ -38,16 +43,15 @@ def tile_attend_bgroupshare_heads_kernel(tc, hid, voc_words, voc_scales, target,
         for quad in range(4):
             nc.sync.dma_start(
                 planes[32 * quad : 32 * quad + 16, :].bitcast(I32),
-                voc_scales[0][4 * quad : 4 * quad + 4, :].rearrange("r (c n) -> c r n", c=CH).bitcast(I32),
+                voc_scales[0][4 * quad : 4 * quad + 4, :].rearrange("r (c n) -> c r n", c=BANKS).bitcast(I32),
             )
 
         flat_words = voc_words[0].rearrange("p n t -> p (n t)")
-        word_of = {}
+        words = []
         for first, width in WORD_LOADS:
             wt = sb.tile([P, width], U32, name="words%d" % first, align_bytes=64)
             nc.sync.dma_start(wt[:].bitcast(I32), flat_words[:, PACK * first : PACK * (first + width)].bitcast(I32))
-            for c0 in range(0, width, N):
-                word_of[(first + c0) // N] = wt[:, c0 : c0 + N]
+            words.append(wt)
 
         offsets = sb.tile([P, I // 16], U16, name="offsets")
         nc.sync.dma_start(offsets[:], offs)
@@ -71,12 +75,17 @@ def tile_attend_bgroupshare_heads_kernel(tc, hid, voc_words, voc_scales, target,
         nc.vector.memset(s2[:], 0.0)
         f = sb.tile([P, CH], F32, name="f")
         nc.vector.memset(f[:, CH - 1 : CH], 1.0)
+        ones = sb.tile([P, I], F32, name="ones")
+        nc.gpsimd.memset(ones[:], 1.0)
 
         hid_bf = sb.tile([P, Q, PACK], BF16, name="hid_bf", align_bytes=64)
-        nc.vector.tensor_copy(hid_bf[:], hid_raw[:].rearrange("p j q -> p q j"))
         hid_codes = sb.tile([P, Q], U32, name="hid_codes", align_bytes=64)
         hid_scales = sb.tile([P, Q], U8, name="hid_scales", align_bytes=64)
-        nc.vector.quantize_mx(out=hid_codes[:].bitcast(FP8X4), scales=hid_scales[:], in_=hid_bf[:].rearrange("p q j -> p (q j)"))
+        q_halves = [slice(0, Q // 2), slice(Q // 2, Q)]
+        for qs in q_halves:
+            nc.vector.tensor_copy(hid_bf[:, qs, :], hid_raw[:, :, qs].rearrange("p j q -> p q j"))
+        for qs in q_halves:
+            nc.vector.quantize_mx(out=hid_codes[:, qs].bitcast(FP8X4), scales=hid_scales[:, qs], in_=hid_bf[:, qs, :].rearrange("p q j -> p (q j)"))
 
         tsum = sb.tile([P, 1], F32, name="tsum")
         tneg = sb.tile([P, G], F32, name="tneg")
@@ -87,35 +96,40 @@ def tile_attend_bgroupshare_heads_kernel(tc, hid, voc_words, voc_scales, target,
         mx = sb.tile([P, CH], F32, name="mx")
         zc = sb.tile([P, CH], F32, name="zc")
         nm1 = sb.tile([P, 1], F32, name="nm1")
-        for c in range(CH):
-            cols = slice(c * N, (c + 1) * N)
-            bank = ps.tile([P, N], F32, name="bank%d" % c)
-            nc.tensor.matmul_mx(
-                out=bank[:],
-                lhsT=hid_codes[:].bitcast(FP8X4),
-                lhsT_scale=hid_scales[:],
-                rhs=word_of[c].bitcast(FP8X4),
-                rhs_scale=planes[4 * c : P, :],
-                start=True,
-                stop=True,
-            )
-            nc.vector.tensor_scalar(a[:, cols], bank[:], 1.0, None, ALU.mult, ALU.max, accum_out=mx[:, c : c + 1])
+        banks = [ps.tile([P, N], F32, name="bank%d" % b) for b in range(BANKS)]
+        for c, (first, width) in enumerate(SCORE_CHUNKS):
+            b = first // N
+            cols = slice(first, first + width)
+            inside = slice(first % N, first % N + width)
+            for wt, (w0, wn) in zip(words, WORD_LOADS):
+                lo, hi = max(first, w0), min(first + width, w0 + wn)
+                if lo < hi:
+                    nc.tensor.matmul_mx(
+                        out=banks[b][:, lo - b * N : hi - b * N],
+                        lhsT=hid_codes[:].bitcast(FP8X4),
+                        lhsT_scale=hid_scales[:],
+                        rhs=wt[:, lo - w0 : hi - w0].bitcast(FP8X4),
+                        rhs_scale=planes[4 * b : P, lo - b * N : hi - b * N],
+                        start=True,
+                        stop=True,
+                    )
+            nc.vector.tensor_scalar(a[:, cols], banks[b][:, inside], 1.0, None, ALU.mult, ALU.max, accum_out=mx[:, c : c + 1])
             if c < CH - 1:
                 nm = sb.tile([P, 1], F32, name="nm%d" % c)
                 nc.gpsimd.tensor_scalar(nm[:], mx[:, c : c + 1], -1.0, 0.0, ALU.mult, ALU.add)
-            else:
-                nm = nm1
-                nc.vector.tensor_reduce(nm1[:], mx[:], AX.X, ALU.max, negate=True)
-                nc.scalar.activation(f[:, : CH - 1], mx[:, : CH - 1], ACT.Exp, bias=nm1[:])
-            nc.scalar.activation(p[:, cols], a[:, cols], ACT.Exp, bias=nm[:], accum_out=zc[:, c : c + 1])
+                nc.scalar.activation(p[:, cols], a[:, cols], ACT.Exp, bias=nm[:], accum_out=zc[:, c : c + 1])
+        nc.vector.tensor_reduce(nm1[:], mx[:], AX.X, ALU.max, negate=True)
+        last = slice(SCORE_CHUNKS[-1][0], SCORE_CHUNKS[-1][0] + SCORE_CHUNKS[-1][1])
+        nc.scalar.activation(p[:, last], a[:, last], ACT.Exp, bias=nm1[:], accum_out=zc[:, CH - 1 : CH])
 
         ax = sb.tile([P, I], F32, name="ax")
-        nc.vector.tensor_copy(ax[:], a[:].indirect(offsets[:]))
-        H = I // 2
-        GH = G // 2
         px = sb.tile([P, I], F32, name="px")
-        for h in range(2):
-            nc.scalar.activation(px[:, h * H : (h + 1) * H], ax[:, h * H : (h + 1) * H], ACT.Exp, bias=nm1[:])
+        for k, (first, width) in enumerate(LIST_PIECES):
+            slots = slice(first, first + width)
+            nc.vector.tensor_tensor(ax[:, slots], a[:].indirect(offsets[:, first // 16 : (first + width) // 16]), ones[:, slots], ALU.mult)
+            nc.scalar.activation(px[:, slots], ax[:, slots], ACT.Exp, bias=nm1[:])
+            if k == 0:
+                nc.scalar.activation(f[:, : CH - 1], mx[:, : CH - 1], ACT.Exp, bias=nm1[:])
 
         zf = sb.tile([P, CH], F32, name="zf")
         z = sb.tile([P, 1], F32, name="z")
@@ -126,48 +140,60 @@ def tile_attend_bgroupshare_heads_kernel(tc, hid, voc_words, voc_scales, target,
         nc.vector.tensor_scalar(cf[:], f[:], rz[:], tsum[:], ALU.mult, ALU.mult)
 
         gs = sb.tile([P, G], F32, name="gs")
-        rg = sb.tile([P, G], F32, name="rg")
-        r1 = sb.tile([P, I], F32, name="r1")
-        for h in range(2):
-            nc.vector.tensor_reduce(gs[:, h * GH : (h + 1) * GH], px[:, h * H : (h + 1) * H].rearrange("p (g j) -> p g j", j=GROUP), AX.X, ALU.add)
-        for h in range(2):
-            nc.vector.reciprocal(rg[:, h * GH : (h + 1) * GH], gs[:, h * GH : (h + 1) * GH])
-        for h in range(2):
+        rg = sb.tile([P, G], F32, name="rg", tag="rg")
+        r1s = {}
+        def group_sum(first, width):
+            groups = slice(first // GROUP, (first + width) // GROUP)
+            nc.vector.tensor_reduce(gs[:, groups], px[:, first : first + width].rearrange("p (g j) -> p g j", j=GROUP), AX.X, ALU.add)
+        def recip(first, width):
+            groups = slice(first // GROUP, (first + width) // GROUP)
+            nc.vector.reciprocal(rg[:, groups], gs[:, groups])
+        def spread(first, width):
+            groups = slice(first // GROUP, (first + width) // GROUP)
+            shape = [P, width // GROUP, GROUP]
+            r1 = sb.tile([P, width], F32, name="r1_%d" % first, tag="r1_%d" % first)
+            r1s.setdefault(first, r1)
             nc.vector.scalar_tensor_tensor(
-                r1[:, h * H : (h + 1) * H].rearrange("p (g j) -> p g j", j=GROUP),
-                rg[:, h * GH : (h + 1) * GH].unsqueeze(2).to_broadcast([P, GH, GROUP]),
+                r1[:].rearrange("p (g j) -> p g j", j=GROUP),
+                rg[:, groups].unsqueeze(2).to_broadcast(shape),
                 OUT_SCALE,
-                tgt[:, h * GH : (h + 1) * GH].unsqueeze(2).to_broadcast([P, GH, GROUP]),
+                tgt[:, groups].unsqueeze(2).to_broadcast(shape),
                 ALU.mult,
                 ALU.mult,
             )
-        nc.vector.tensor_tensor(s2[:].indirect(offsets[:]), px[:], r1[:], ALU.mult)
+        def scatter(first, width):
+            nc.vector.tensor_tensor(s2[:].indirect(offsets[:, first // 16 : (first + width) // 16]), px[:, first : first + width], r1s[first][:], ALU.mult)
+        for step in (group_sum, recip, spread):
+            for piece in LIST_PIECES:
+                step(*piece)
+        scatter(*LIST_PIECES[0])
+        direct = sb.tile([P, DIRECT], F32, name="direct", tag="rg")
+        nc.vector.scalar_tensor_tensor(direct[:], p[:, :DIRECT], cf[:, 0:1], olds[0][:, :DIRECT], ALU.mult, ALU.add)
+        scatter(*LIST_PIECES[1])
 
-        turned = []
+        turned = [ps.tile([P, N], F32, name="turned%d" % b) for b in range(BANKS)]
+        for col in range(DIRECT, V, P):
+            nc.tensor.matmul(turned[col // N][:, col % N : col % N + P], olds[col // (V // 2)][:, col % (V // 2) : col % (V // 2) + P], ident[:], start=(col == DIRECT or col % N == 0), stop=False, is_transpose=True)
+        cp = sb.tile([P, V], F32, name="cp")
         for c in range(CH):
-            tb = ps.tile([P, N], F32, name="turned%d" % c)
-            for j in range(N // P):
-                o0 = (c % 2) * N + j * P
-                nc.tensor.matmul(tb[:, j * P : (j + 1) * P], olds[c // 2][:, o0 : o0 + P], ident[:], start=(j == 0), stop=False, is_transpose=True)
-            turned.append(tb)
-        for c in range(CH):
-            cols = slice(c * N, (c + 1) * N)
-            cp = sb.tile([P, N], F32, name="cp%d" % c)
-            nc.scalar.activation(cp[:], p[:, cols], ACT.Copy, scale=cf[:, c : c + 1])
-            for j in range(N // P):
-                nc.tensor.matmul(turned[c][:, j * P : (j + 1) * P], cp[:, j * P : (j + 1) * P], ident[:], start=False, stop=(j == N // P - 1), is_transpose=True)
+            lo, hi = max(c * N, DIRECT), (c + 1) * N
+            nc.scalar.activation(cp[:, lo:hi], p[:, lo:hi], ACT.Copy, scale=cf[:, c : c + 1])
+            for col in range(lo, hi, P):
+                nc.tensor.matmul(turned[c][:, col % N : col % N + P], cp[:, col : col + P], ident[:], start=False, stop=(col % N == N - P), is_transpose=True)
         backs = []
-        for c in range(CH):
-            wt = sb.tile([P, N], F32, name="wt%d" % c)
-            nc.scalar.copy(wt[:], turned[c][:])
-            back = ps.tile([P, N], F32, name="bank%d" % c)
-            for j in range(N // P):
-                nc.tensor.transpose(back[:, j * P : (j + 1) * P], wt[:, j * P : (j + 1) * P], ident[:])
+        for b in range(BANKS):
+            lo = max(b * N, DIRECT) - b * N
+            wt = sb.tile([P, N], F32, name="wt%d" % b)
+            nc.scalar.copy(wt[:, lo:], turned[b][:, lo:])
+            back = ps.tile([P, N], F32, name="bank%d" % b)
+            for j in range(lo, N, P):
+                nc.tensor.transpose(back[:, j : j + P], wt[:, j : j + P], ident[:])
             backs.append(back)
         first = 0
-        for k, width in enumerate([128, 384, 512, 512, 384, 128]):
+        for k, width in enumerate(STORE_WIDTHS):
             cols = slice(first, first + width)
             res = sb.tile([P, width], F32, name="res%d" % k)
-            nc.vector.tensor_tensor(res[:], backs[first // N][:, first % N : first % N + width], s2[:, cols], ALU.add)
+            dense = direct[:, cols] if first < DIRECT else backs[first // N][:, first % N : first % N + width]
+            nc.vector.tensor_tensor(res[:], dense, s2[:, cols], ALU.add)
             (nc.sync if k % 2 == 0 else nc.scalar).dma_start(out[:, cols], res[:])
             first = first + width

@@ -17,21 +17,22 @@ AX = mybir.AxisListType
 P = 128
 D, V, Q, I, G = 512, 2048, 128, 512, 64
 PACK = 4
+QUADRANTS = 4
 GROUP = I // G
+STRIPE = 16
 N = 512
-BANKS = V // N
+CHUNKS = V // N
 OUT_SCALE = 64.0
 FLOPS = 2 * D * Q * V
-SCORE_CHUNKS = [(0, 512), (512, 512), (1024, 512), (1536, 512)]
-WORD_LOADS = [(0, 512), (512, 768), (1280, 768)]
-LIST_PIECES = [(0, 256), (256, 256)]
+
+REST = (V - N) // 2
+WORD_LOADS = [(0, N), (N, REST), (N + REST, REST)]
+LIST_HALVES = [(0, I // 2), (I // 2, I // 2)]
 DIRECT = 256
-STORE_WIDTHS = [256, 256, 512, 512, 512]
 
 
 def tile_attend_bgroupshare_heads_kernel(tc, hid, voc_words, voc_scales, target, old, offs, out):
     nc = tc.nc
-    CH = len(SCORE_CHUNKS)
     with ExitStack() as ctx:
         sb = ctx.enter_context(tc.tile_pool(name="sb", bufs=1))
         ps = ctx.enter_context(tc.psum_pool(name="ps", bufs=1))
@@ -39,42 +40,41 @@ def tile_attend_bgroupshare_heads_kernel(tc, hid, voc_words, voc_scales, target,
         hid_raw = sb.tile([P, PACK, Q], F32, name="hid_raw")
         nc.sync.dma_start(hid_raw[:], hid.rearrange("(p j) q -> p j q", j=PACK))
 
-        planes = sb.tile([P, N], U8, name="planes", align_bytes=64)
-        for quad in range(4):
+        voc_planes = sb.tile([P, N], U8, name="voc_planes", align_bytes=64)
+        for quad in range(QUADRANTS):
             nc.sync.dma_start(
-                planes[32 * quad : 32 * quad + 16, :].bitcast(I32),
-                voc_scales[0][4 * quad : 4 * quad + 4, :].rearrange("r (c n) -> c r n", c=BANKS).bitcast(I32),
+                voc_planes[32 * quad : 32 * quad + 4 * CHUNKS, :].bitcast(I32),
+                voc_scales[0][4 * quad : 4 * quad + 4, :].rearrange("r (c n) -> c r n", c=CHUNKS).bitcast(I32),
             )
 
-        flat_words = voc_words[0].rearrange("p n t -> p (n t)")
-        words = []
+        word_bytes = voc_words[0].rearrange("p n t -> p (n t)")
+        word_tiles = []
         for first, width in WORD_LOADS:
-            wt = sb.tile([P, width], U32, name="words%d" % first, align_bytes=64)
-            nc.sync.dma_start(wt[:].bitcast(I32), flat_words[:, PACK * first : PACK * (first + width)].bitcast(I32))
-            words.append(wt)
+            words = sb.tile([P, width], U32, name="words%d" % first, align_bytes=64)
+            nc.sync.dma_start(words[:].bitcast(I32), word_bytes[:, PACK * first : PACK * (first + width)].bitcast(I32))
+            word_tiles.append(words)
 
-        offsets = sb.tile([P, I // 16], U16, name="offsets")
+        offsets = sb.tile([P, I // STRIPE], U16, name="offsets")
         nc.sync.dma_start(offsets[:], offs)
         tgt = sb.tile([P, G], F32, name="tgt")
         nc.sync.dma_start(tgt[:], target)
-        olds = []
+        half_v = V // 2
+        old_halves = []
         for h in range(2):
-            ot = sb.tile([P, V // 2], F32, name="old%d" % h)
-            nc.sync.dma_start(ot[:], old[:, h * (V // 2) : (h + 1) * (V // 2)])
-            olds.append(ot)
+            old_half = sb.tile([P, half_v], F32, name="old%d" % h)
+            nc.sync.dma_start(old_half[:], old[:, h * half_v : (h + 1) * half_v])
+            old_halves.append(old_half)
 
-        warm = sb.tile([P, 1], F32, name="warm")
-        nc.vector.memset(warm[:], 0.0)
-        warm_out = sb.tile([P, 1], F32, name="warm_out")
-        nc.scalar.activation(warm_out[:], warm[:], ACT.Exp)
+        zero = sb.tile([P, 1], F32, name="zero")
+        nc.vector.memset(zero[:], 0.0)
+        factor = sb.tile([P, CHUNKS], F32, name="factor")
+        nc.scalar.activation(factor[:, CHUNKS - 1 :], zero[:], ACT.Exp)
 
         ident = sb.tile([P, P], F32, name="ident")
         make_identity(nc, ident[:])
 
-        s2 = sb.tile([P, V], F32, name="s2")
-        nc.vector.memset(s2[:], 0.0)
-        f = sb.tile([P, CH], F32, name="f")
-        nc.vector.memset(f[:, CH - 1 : CH], 1.0)
+        listed = sb.tile([P, V], F32, name="listed")
+        nc.vector.memset(listed[:], 0.0)
         ones = sb.tile([P, I], F32, name="ones")
         nc.gpsimd.memset(ones[:], 1.0)
 
@@ -85,115 +85,146 @@ def tile_attend_bgroupshare_heads_kernel(tc, hid, voc_words, voc_scales, target,
         for qs in q_halves:
             nc.vector.tensor_copy(hid_bf[:, qs, :], hid_raw[:, :, qs].rearrange("p j q -> p q j"))
         for qs in q_halves:
-            nc.vector.quantize_mx(out=hid_codes[:, qs].bitcast(FP8X4), scales=hid_scales[:, qs], in_=hid_bf[:, qs, :].rearrange("p q j -> p (q j)"))
+            nc.vector.quantize_mx(
+                out=hid_codes[:, qs].bitcast(FP8X4),
+                scales=hid_scales[:, qs],
+                in_=hid_bf[:, qs, :].rearrange("p q j -> p (q j)"),
+            )
 
-        tsum = sb.tile([P, 1], F32, name="tsum")
-        tneg = sb.tile([P, G], F32, name="tneg")
-        nc.scalar.activation(tneg[:], tgt[:], ACT.Copy, scale=-1.0, accum_out=tsum[:])
+        neg_t = sb.tile([P, 1], F32, name="neg_t")
+        neg_tgt = sb.tile([P, G], F32, name="neg_tgt")
+        nc.scalar.activation(neg_tgt[:], tgt[:], ACT.Copy, scale=-1.0, accum_out=neg_t[:])
 
         a = sb.tile([P, V], F32, name="a")
         p = sb.tile([P, V], F32, name="p")
-        mx = sb.tile([P, CH], F32, name="mx")
-        zc = sb.tile([P, CH], F32, name="zc")
-        nm1 = sb.tile([P, 1], F32, name="nm1")
-        banks = [ps.tile([P, N], F32, name="bank%d" % b) for b in range(BANKS)]
-        for c, (first, width) in enumerate(SCORE_CHUNKS):
-            b = first // N
-            cols = slice(first, first + width)
-            inside = slice(first % N, first % N + width)
-            for wt, (w0, wn) in zip(words, WORD_LOADS):
-                lo, hi = max(first, w0), min(first + width, w0 + wn)
+        chunk_max = sb.tile([P, CHUNKS], F32, name="chunk_max")
+        chunk_sum = sb.tile([P, CHUNKS], F32, name="chunk_sum")
+        neg_m1 = sb.tile([P, 1], F32, name="neg_m1")
+        score_banks = [ps.tile([P, N], F32, name="bank%d" % c) for c in range(CHUNKS)]
+        for c in range(CHUNKS):
+            base = c * N
+            cols = slice(base, base + N)
+            for words, (first, width) in zip(word_tiles, WORD_LOADS):
+                lo, hi = max(base, first), min(base + N, first + width)
                 if lo < hi:
                     nc.tensor.matmul_mx(
-                        out=banks[b][:, lo - b * N : hi - b * N],
+                        out=score_banks[c][:, lo - base : hi - base],
                         lhsT=hid_codes[:].bitcast(FP8X4),
                         lhsT_scale=hid_scales[:],
-                        rhs=wt[:, lo - w0 : hi - w0].bitcast(FP8X4),
-                        rhs_scale=planes[4 * b : P, lo - b * N : hi - b * N],
+                        rhs=words[:, lo - first : hi - first].bitcast(FP8X4),
+                        rhs_scale=voc_planes[4 * c : P, lo - base : hi - base],
                         start=True,
                         stop=True,
                     )
-            nc.vector.tensor_scalar(a[:, cols], banks[b][:, inside], 1.0, None, ALU.mult, ALU.max, accum_out=mx[:, c : c + 1])
-            if c < CH - 1:
-                nm = sb.tile([P, 1], F32, name="nm%d" % c)
-                nc.gpsimd.tensor_scalar(nm[:], mx[:, c : c + 1], -1.0, 0.0, ALU.mult, ALU.add)
-                nc.scalar.activation(p[:, cols], a[:, cols], ACT.Exp, bias=nm[:], accum_out=zc[:, c : c + 1])
-        nc.vector.tensor_reduce(nm1[:], mx[:], AX.X, ALU.max, negate=True)
-        last = slice(SCORE_CHUNKS[-1][0], SCORE_CHUNKS[-1][0] + SCORE_CHUNKS[-1][1])
-        nc.scalar.activation(p[:, last], a[:, last], ACT.Exp, bias=nm1[:], accum_out=zc[:, CH - 1 : CH])
+            nc.vector.tensor_scalar(
+                a[:, cols], score_banks[c][:], 1.0, None, ALU.mult, ALU.max, accum_out=chunk_max[:, c : c + 1]
+            )
+            if c < CHUNKS - 1:
+                neg_max = sb.tile([P, 1], F32, name="neg_max%d" % c)
+                nc.gpsimd.tensor_scalar(neg_max[:], chunk_max[:, c : c + 1], -1.0, 0.0, ALU.mult, ALU.add)
+                nc.scalar.activation(
+                    p[:, cols], a[:, cols], ACT.Exp, bias=neg_max[:], accum_out=chunk_sum[:, c : c + 1]
+                )
+        nc.vector.tensor_reduce(neg_m1[:], chunk_max[:], AX.X, ALU.max, negate=True)
+        nc.scalar.activation(
+            p[:, V - N :], a[:, V - N :], ACT.Exp, bias=neg_m1[:], accum_out=chunk_sum[:, CHUNKS - 1 :]
+        )
+
+        def list_part(first, width):
+            return offsets[:, first // STRIPE : (first + width) // STRIPE]
 
         ax = sb.tile([P, I], F32, name="ax")
         px = sb.tile([P, I], F32, name="px")
-        for k, (first, width) in enumerate(LIST_PIECES):
+        for first, width in LIST_HALVES:
             slots = slice(first, first + width)
-            nc.vector.tensor_tensor(ax[:, slots], a[:].indirect(offsets[:, first // 16 : (first + width) // 16]), ones[:, slots], ALU.mult)
-            nc.scalar.activation(px[:, slots], ax[:, slots], ACT.Exp, bias=nm1[:])
-            if k == 0:
-                nc.scalar.activation(f[:, : CH - 1], mx[:, : CH - 1], ACT.Exp, bias=nm1[:])
+            nc.vector.tensor_tensor(ax[:, slots], a[:].indirect(list_part(first, width)), ones[:, slots], ALU.mult)
+            nc.scalar.activation(px[:, slots], ax[:, slots], ACT.Exp, bias=neg_m1[:])
+            if first == 0:
+                nc.scalar.activation(factor[:, : CHUNKS - 1], chunk_max[:, : CHUNKS - 1], ACT.Exp, bias=neg_m1[:])
 
-        zf = sb.tile([P, CH], F32, name="zf")
-        z = sb.tile([P, 1], F32, name="z")
-        nc.vector.scalar_tensor_tensor(zf[:], zc[:], 1.0 / OUT_SCALE, f[:], ALU.mult, ALU.mult, accum_out=z[:])
-        rz = sb.tile([P, 1], F32, name="rz")
-        nc.vector.reciprocal(rz[:], z[:])
-        cf = sb.tile([P, CH], F32, name="cf")
-        nc.vector.tensor_scalar(cf[:], f[:], rz[:], tsum[:], ALU.mult, ALU.mult)
+        sum_terms = sb.tile([P, CHUNKS], F32, name="sum_terms")
+        z_scaled = sb.tile([P, 1], F32, name="z_scaled")
+        nc.vector.scalar_tensor_tensor(
+            sum_terms[:], chunk_sum[:], 1.0 / OUT_SCALE, factor[:], ALU.mult, ALU.mult, accum_out=z_scaled[:]
+        )
+        inv_z = sb.tile([P, 1], F32, name="inv_z")
+        nc.vector.reciprocal(inv_z[:], z_scaled[:])
+        coeff = sb.tile([P, CHUNKS], F32, name="coeff")
+        nc.vector.tensor_scalar(coeff[:], factor[:], inv_z[:], neg_t[:], ALU.mult, ALU.mult)
 
-        gs = sb.tile([P, G], F32, name="gs")
-        rg = sb.tile([P, G], F32, name="rg", tag="rg")
-        r1s = {}
-        def group_sum(first, width):
-            groups = slice(first // GROUP, (first + width) // GROUP)
-            nc.vector.tensor_reduce(gs[:, groups], px[:, first : first + width].rearrange("p (g j) -> p g j", j=GROUP), AX.X, ALU.add)
-        def recip(first, width):
-            groups = slice(first // GROUP, (first + width) // GROUP)
-            nc.vector.reciprocal(rg[:, groups], gs[:, groups])
-        def spread(first, width):
-            groups = slice(first // GROUP, (first + width) // GROUP)
-            shape = [P, width // GROUP, GROUP]
-            r1 = sb.tile([P, width], F32, name="r1_%d" % first, tag="r1_%d" % first)
-            r1s.setdefault(first, r1)
+        group_sum = sb.tile([P, G], F32, name="group_sum")
+        inv_sum = sb.tile([P, G], F32, name="inv_sum", tag="inv_sum_then_direct")
+        group_halves = [slice(first // GROUP, (first + width) // GROUP) for first, width in LIST_HALVES]
+        for (first, width), groups in zip(LIST_HALVES, group_halves):
+            nc.vector.tensor_reduce(
+                group_sum[:, groups],
+                px[:, first : first + width].rearrange("p (g j) -> p g j", j=GROUP),
+                AX.X,
+                ALU.add,
+            )
+        for groups in group_halves:
+            nc.vector.reciprocal(inv_sum[:, groups], group_sum[:, groups])
+        weights = []
+        for (first, width), groups in zip(LIST_HALVES, group_halves):
+            spread = [P, width // GROUP, GROUP]
+            weight = sb.tile([P, width], F32, name="weight%d" % first)
             nc.vector.scalar_tensor_tensor(
-                r1[:].rearrange("p (g j) -> p g j", j=GROUP),
-                rg[:, groups].unsqueeze(2).to_broadcast(shape),
+                weight[:].rearrange("p (g j) -> p g j", j=GROUP),
+                inv_sum[:, groups].unsqueeze(2).to_broadcast(spread),
                 OUT_SCALE,
-                tgt[:, groups].unsqueeze(2).to_broadcast(shape),
+                tgt[:, groups].unsqueeze(2).to_broadcast(spread),
                 ALU.mult,
                 ALU.mult,
             )
-        def scatter(first, width):
-            nc.vector.tensor_tensor(s2[:].indirect(offsets[:, first // 16 : (first + width) // 16]), px[:, first : first + width], r1s[first][:], ALU.mult)
-        for step in (group_sum, recip, spread):
-            for piece in LIST_PIECES:
-                step(*piece)
-        scatter(*LIST_PIECES[0])
-        direct = sb.tile([P, DIRECT], F32, name="direct", tag="rg")
-        nc.vector.scalar_tensor_tensor(direct[:], p[:, :DIRECT], cf[:, 0:1], olds[0][:, :DIRECT], ALU.mult, ALU.add)
-        scatter(*LIST_PIECES[1])
+            weights.append(weight)
 
-        turned = [ps.tile([P, N], F32, name="turned%d" % b) for b in range(BANKS)]
+        def scatter(h):
+            first, width = LIST_HALVES[h]
+            nc.vector.tensor_tensor(
+                listed[:].indirect(list_part(first, width)), px[:, first : first + width], weights[h][:], ALU.mult
+            )
+
+        scatter(0)
+        direct = sb.tile([P, DIRECT], F32, name="direct", tag="inv_sum_then_direct")
+        nc.vector.scalar_tensor_tensor(
+            direct[:], p[:, :DIRECT], coeff[:, 0:1], old_halves[0][:, :DIRECT], ALU.mult, ALU.add
+        )
+        scatter(1)
+
+        turned = [ps.tile([P, N], F32, name="turned%d" % c) for c in range(CHUNKS)]
         for col in range(DIRECT, V, P):
-            nc.tensor.matmul(turned[col // N][:, col % N : col % N + P], olds[col // (V // 2)][:, col % (V // 2) : col % (V // 2) + P], ident[:], start=(col == DIRECT or col % N == 0), stop=False, is_transpose=True)
-        cp = sb.tile([P, V], F32, name="cp")
-        for c in range(CH):
-            lo, hi = max(c * N, DIRECT), (c + 1) * N
-            nc.scalar.activation(cp[:, lo:hi], p[:, lo:hi], ACT.Copy, scale=cf[:, c : c + 1])
+            nc.tensor.matmul(
+                turned[col // N][:, col % N : col % N + P],
+                old_halves[col // half_v][:, col % half_v : col % half_v + P],
+                ident[:],
+                start=(col == DIRECT or col % N == 0),
+                stop=False,
+                is_transpose=True,
+            )
+        spans = [(max(c * N, DIRECT), (c + 1) * N) for c in range(CHUNKS)]
+        scaled_p = sb.tile([P, V], F32, name="scaled_p")
+        for c, (lo, hi) in enumerate(spans):
+            nc.scalar.activation(scaled_p[:, lo:hi], p[:, lo:hi], ACT.Copy, scale=coeff[:, c : c + 1])
             for col in range(lo, hi, P):
-                nc.tensor.matmul(turned[c][:, col % N : col % N + P], cp[:, col : col + P], ident[:], start=False, stop=(col % N == N - P), is_transpose=True)
-        backs = []
-        for b in range(BANKS):
-            lo = max(b * N, DIRECT) - b * N
-            wt = sb.tile([P, N], F32, name="wt%d" % b)
-            nc.scalar.copy(wt[:, lo:], turned[b][:, lo:])
-            back = ps.tile([P, N], F32, name="bank%d" % b)
-            for j in range(lo, N, P):
-                nc.tensor.transpose(back[:, j : j + P], wt[:, j : j + P], ident[:])
-            backs.append(back)
-        first = 0
-        for k, width in enumerate(STORE_WIDTHS):
-            cols = slice(first, first + width)
-            res = sb.tile([P, width], F32, name="res%d" % k)
-            dense = direct[:, cols] if first < DIRECT else backs[first // N][:, first % N : first % N + width]
-            nc.vector.tensor_tensor(res[:], dense, s2[:, cols], ALU.add)
-            (nc.sync if k % 2 == 0 else nc.scalar).dma_start(out[:, cols], res[:])
-            first = first + width
+                nc.tensor.matmul(
+                    turned[c][:, col % N : col % N + P],
+                    scaled_p[:, col : col + P],
+                    ident[:],
+                    start=False,
+                    stop=(col + P == hi),
+                    is_transpose=True,
+                )
+        pieces = [(0, DIRECT, direct[:])]
+        for c, (lo, hi) in enumerate(spans):
+            inside = lo % N
+            turned_sb = sb.tile([P, N], F32, name="turned_sb%d" % c)
+            nc.scalar.copy(turned_sb[:, inside:], turned[c][:, inside:])
+            dense_bank = ps.tile([P, N], F32, name="bank%d" % c)
+            for j in range(inside, N, P):
+                nc.tensor.transpose(dense_bank[:, j : j + P], turned_sb[:, j : j + P], ident[:])
+            pieces.append((lo, hi, dense_bank[:, inside:]))
+
+        for k, (lo, hi, dense) in enumerate(pieces):
+            result = sb.tile([P, hi - lo], F32, name="result%d" % k)
+            nc.vector.tensor_tensor(result[:], dense, listed[:, lo:hi], ALU.add)
+            (nc.sync if k % 2 == 0 else nc.scalar).dma_start(out[:, lo:hi], result[:])

from contextlib import ExitStack

import concourse.mybir as mybir
from concourse.masks import make_identity

F32 = mybir.dt.float32
BF16 = mybir.dt.bfloat16
I32 = mybir.dt.int32
U32 = mybir.dt.uint32
U16 = mybir.dt.uint16
U8 = mybir.dt.uint8
FP8X4 = mybir.dt.float8_e4m3fn_x4
ALU = mybir.AluOpType
ACT = mybir.ActivationFunctionType
AX = mybir.AxisListType

P = 128
D, V, Q, I, G = 512, 2048, 128, 512, 64
PACK = 4
QUADRANTS = 4
GROUP = I // G
STRIPE = 16
N = 512
CHUNKS = V // N
OUT_SCALE = 64.0
FLOPS = 2 * D * Q * V

REST = (V - N) // 2
WORD_LOADS = [(0, N), (N, REST), (N + REST, REST)]
LIST_HALVES = [(0, I // 2), (I // 2, I // 2)]
DIRECT = 256


def tile_attend_bgroupshare_heads_kernel(tc, hid, voc_words, voc_scales, target, old, offs, out):
    nc = tc.nc
    with ExitStack() as ctx:
        sb = ctx.enter_context(tc.tile_pool(name="sb", bufs=1))
        ps = ctx.enter_context(tc.psum_pool(name="ps", bufs=1))

        hid_raw = sb.tile([P, PACK, Q], F32, name="hid_raw")
        nc.sync.dma_start(hid_raw[:], hid.rearrange("(p j) q -> p j q", j=PACK))

        voc_planes = sb.tile([P, N], U8, name="voc_planes", align_bytes=64)
        for quad in range(QUADRANTS):
            nc.sync.dma_start(
                voc_planes[32 * quad : 32 * quad + 4 * CHUNKS, :].bitcast(I32),
                voc_scales[0][4 * quad : 4 * quad + 4, :].rearrange("r (c n) -> c r n", c=CHUNKS).bitcast(I32),
            )

        word_bytes = voc_words[0].rearrange("p n t -> p (n t)")
        word_tiles = []
        for first, width in WORD_LOADS:
            words = sb.tile([P, width], U32, name="words%d" % first, align_bytes=64)
            nc.sync.dma_start(words[:].bitcast(I32), word_bytes[:, PACK * first : PACK * (first + width)].bitcast(I32))
            word_tiles.append(words)

        offsets = sb.tile([P, I // STRIPE], U16, name="offsets")
        nc.sync.dma_start(offsets[:], offs)
        tgt = sb.tile([P, G], F32, name="tgt")
        nc.sync.dma_start(tgt[:], target)
        half_v = V // 2
        old_halves = []
        for h in range(2):
            old_half = sb.tile([P, half_v], F32, name="old%d" % h)
            nc.sync.dma_start(old_half[:], old[:, h * half_v : (h + 1) * half_v])
            old_halves.append(old_half)

        zero = sb.tile([P, 1], F32, name="zero")
        nc.vector.memset(zero[:], 0.0)
        factor = sb.tile([P, CHUNKS], F32, name="factor")
        nc.scalar.activation(factor[:, CHUNKS - 1 :], zero[:], ACT.Exp)

        ident = sb.tile([P, P], F32, name="ident")
        make_identity(nc, ident[:])

        listed = sb.tile([P, V], F32, name="listed")
        nc.vector.memset(listed[:], 0.0)
        ones = sb.tile([P, I], F32, name="ones")
        nc.gpsimd.memset(ones[:], 1.0)

        hid_bf = sb.tile([P, Q, PACK], BF16, name="hid_bf", align_bytes=64)
        hid_codes = sb.tile([P, Q], U32, name="hid_codes", align_bytes=64)
        hid_scales = sb.tile([P, Q], U8, name="hid_scales", align_bytes=64)
        q_halves = [slice(0, Q // 2), slice(Q // 2, Q)]
        for qs in q_halves:
            nc.vector.tensor_copy(hid_bf[:, qs, :], hid_raw[:, :, qs].rearrange("p j q -> p q j"))
        for qs in q_halves:
            nc.vector.quantize_mx(
                out=hid_codes[:, qs].bitcast(FP8X4),
                scales=hid_scales[:, qs],
                in_=hid_bf[:, qs, :].rearrange("p q j -> p (q j)"),
            )

        neg_t = sb.tile([P, 1], F32, name="neg_t")
        neg_tgt = sb.tile([P, G], F32, name="neg_tgt")
        nc.scalar.activation(neg_tgt[:], tgt[:], ACT.Copy, scale=-1.0, accum_out=neg_t[:])

        a = sb.tile([P, V], F32, name="a")
        p = sb.tile([P, V], F32, name="p")
        chunk_max = sb.tile([P, CHUNKS], F32, name="chunk_max")
        chunk_sum = sb.tile([P, CHUNKS], F32, name="chunk_sum")
        neg_m1 = sb.tile([P, 1], F32, name="neg_m1")
        score_banks = [ps.tile([P, N], F32, name="bank%d" % c) for c in range(CHUNKS)]
        for c in range(CHUNKS):
            base = c * N
            cols = slice(base, base + N)
            for words, (first, width) in zip(word_tiles, WORD_LOADS):
                lo, hi = max(base, first), min(base + N, first + width)
                if lo < hi:
                    nc.tensor.matmul_mx(
                        out=score_banks[c][:, lo - base : hi - base],
                        lhsT=hid_codes[:].bitcast(FP8X4),
                        lhsT_scale=hid_scales[:],
                        rhs=words[:, lo - first : hi - first].bitcast(FP8X4),
                        rhs_scale=voc_planes[4 * c : P, lo - base : hi - base],
                        start=True,
                        stop=True,
                    )
            nc.vector.tensor_scalar(
                a[:, cols], score_banks[c][:], 1.0, None, ALU.mult, ALU.max, accum_out=chunk_max[:, c : c + 1]
            )
            if c < CHUNKS - 1:
                neg_max = sb.tile([P, 1], F32, name="neg_max%d" % c)
                nc.gpsimd.tensor_scalar(neg_max[:], chunk_max[:, c : c + 1], -1.0, 0.0, ALU.mult, ALU.add)
                nc.scalar.activation(
                    p[:, cols], a[:, cols], ACT.Exp, bias=neg_max[:], accum_out=chunk_sum[:, c : c + 1]
                )
        nc.vector.tensor_reduce(neg_m1[:], chunk_max[:], AX.X, ALU.max, negate=True)
        nc.scalar.activation(
            p[:, V - N :], a[:, V - N :], ACT.Exp, bias=neg_m1[:], accum_out=chunk_sum[:, CHUNKS - 1 :]
        )

        def list_part(first, width):
            return offsets[:, first // STRIPE : (first + width) // STRIPE]

        ax = sb.tile([P, I], F32, name="ax")
        px = sb.tile([P, I], F32, name="px")
        for first, width in LIST_HALVES:
            slots = slice(first, first + width)
            nc.vector.tensor_tensor(ax[:, slots], a[:].indirect(list_part(first, width)), ones[:, slots], ALU.mult)
            nc.scalar.activation(px[:, slots], ax[:, slots], ACT.Exp, bias=neg_m1[:])
            if first == 0:
                nc.scalar.activation(factor[:, : CHUNKS - 1], chunk_max[:, : CHUNKS - 1], ACT.Exp, bias=neg_m1[:])

        sum_terms = sb.tile([P, CHUNKS], F32, name="sum_terms")
        z_scaled = sb.tile([P, 1], F32, name="z_scaled")
        nc.vector.scalar_tensor_tensor(
            sum_terms[:], chunk_sum[:], 1.0 / OUT_SCALE, factor[:], ALU.mult, ALU.mult, accum_out=z_scaled[:]
        )
        inv_z = sb.tile([P, 1], F32, name="inv_z")
        nc.vector.reciprocal(inv_z[:], z_scaled[:])
        coeff = sb.tile([P, CHUNKS], F32, name="coeff")
        nc.vector.tensor_scalar(coeff[:], factor[:], inv_z[:], neg_t[:], ALU.mult, ALU.mult)

        group_sum = sb.tile([P, G], F32, name="group_sum")
        inv_sum = sb.tile([P, G], F32, name="inv_sum", tag="inv_sum_then_direct")
        group_halves = [slice(first // GROUP, (first + width) // GROUP) for first, width in LIST_HALVES]
        for (first, width), groups in zip(LIST_HALVES, group_halves):
            nc.vector.tensor_reduce(
                group_sum[:, groups],
                px[:, first : first + width].rearrange("p (g j) -> p g j", j=GROUP),
                AX.X,
                ALU.add,
            )
        for groups in group_halves:
            nc.vector.reciprocal(inv_sum[:, groups], group_sum[:, groups])
        weights = []
        for (first, width), groups in zip(LIST_HALVES, group_halves):
            spread = [P, width // GROUP, GROUP]
            weight = sb.tile([P, width], F32, name="weight%d" % first)
            nc.vector.scalar_tensor_tensor(
                weight[:].rearrange("p (g j) -> p g j", j=GROUP),
                inv_sum[:, groups].unsqueeze(2).to_broadcast(spread),
                OUT_SCALE,
                tgt[:, groups].unsqueeze(2).to_broadcast(spread),
                ALU.mult,
                ALU.mult,
            )
            weights.append(weight)

        def scatter(h):
            first, width = LIST_HALVES[h]
            nc.vector.tensor_tensor(
                listed[:].indirect(list_part(first, width)), px[:, first : first + width], weights[h][:], ALU.mult
            )

        scatter(0)
        direct = sb.tile([P, DIRECT], F32, name="direct", tag="inv_sum_then_direct")
        nc.vector.scalar_tensor_tensor(
            direct[:], p[:, :DIRECT], coeff[:, 0:1], old_halves[0][:, :DIRECT], ALU.mult, ALU.add
        )
        scatter(1)

        turned = [ps.tile([P, N], F32, name="turned%d" % c) for c in range(CHUNKS)]
        for col in range(DIRECT, V, P):
            nc.tensor.matmul(
                turned[col // N][:, col % N : col % N + P],
                old_halves[col // half_v][:, col % half_v : col % half_v + P],
                ident[:],
                start=(col == DIRECT or col % N == 0),
                stop=False,
                is_transpose=True,
            )
        spans = [(max(c * N, DIRECT), (c + 1) * N) for c in range(CHUNKS)]
        scaled_p = sb.tile([P, V], F32, name="scaled_p")
        for c, (lo, hi) in enumerate(spans):
            nc.scalar.activation(scaled_p[:, lo:hi], p[:, lo:hi], ACT.Copy, scale=coeff[:, c : c + 1])
            for col in range(lo, hi, P):
                nc.tensor.matmul(
                    turned[c][:, col % N : col % N + P],
                    scaled_p[:, col : col + P],
                    ident[:],
                    start=False,
                    stop=(col + P == hi),
                    is_transpose=True,
                )
        pieces = [(0, DIRECT, direct[:])]
        for c, (lo, hi) in enumerate(spans):
            inside = lo % N
            turned_sb = sb.tile([P, N], F32, name="turned_sb%d" % c)
            nc.scalar.copy(turned_sb[:, inside:], turned[c][:, inside:])
            dense_bank = ps.tile([P, N], F32, name="bank%d" % c)
            for j in range(inside, N, P):
                nc.tensor.transpose(dense_bank[:, j : j + P], turned_sb[:, j : j + P], ident[:])
            pieces.append((lo, hi, dense_bank[:, inside:]))

        for k, (lo, hi, dense) in enumerate(pieces):
            result = sb.tile([P, hi - lo], F32, name="result%d" % k)
            nc.vector.tensor_tensor(result[:], dense, listed[:, lo:hi], ALU.add)
            (nc.sync if k % 2 == 0 else nc.scalar).dma_start(out[:, lo:hi], result[:])
